import numpy as np
import ml_dtypes


def mxq(x, axis, fmt="e4m3"):
    dtype, down = {"e4m3": (ml_dtypes.float8_e4m3fn, 7), "e5m2": (ml_dtypes.float8_e5m2, 14)}[fmt]
    v = np.moveaxis(np.asarray(x, np.float32).astype(ml_dtypes.bfloat16).astype(np.float64), axis, -1)
    blocks = v.reshape(v.shape[:-1] + (-1, 32))
    amax = np.abs(blocks).max(-1, keepdims=True)
    byte = np.maximum(np.where(amax > 0, np.frexp(amax)[1] - 1 + 127, 0) - down, 1)
    scale = np.exp2(byte - 127.0)
    codes = (blocks / scale).astype(np.float32).astype(dtype).astype(np.float64)
    return np.moveaxis((codes * scale).reshape(v.shape), -1, axis)


WIDE = False


def mx_kscale(k):
    if not WIDE:
        return np.ones(k)
    levels = np.array([10, -10, 5, -5, 0])
    if k % 512:
        return np.exp2(np.random.permutation(np.resize(levels, k // 32))).repeat(32)
    a = np.empty((k // 512, 16))
    for p in range(k // 512):
        a[p, :8] = np.random.permutation(np.resize(levels, 8))
        for g in range(8):
            far = levels[np.abs(levels - a[p, g]) >= 10]
            a[p, g + 8] = far[np.random.randint(len(far))]
    return np.exp2(a.ravel()).repeat(32)


def f64(x):
    return np.asarray(x).astype(np.float64)


def striped(idx):
    return np.tile(np.asarray(idx).reshape(-1, 16).T, (8, 1)).astype(np.uint16)


def unstriped(offs):
    return offs[:16].T.reshape(-1).astype(np.int64)


E2M1 = np.array([0.0, 0.5, 1.0, 1.5, 2.0, 3.0, 4.0, 6.0, -0.0, -0.5, -1.0, -1.5, -2.0, -3.0, -4.0, -6.0])


def pack_weight(w, fmt):
    k, n = w.shape
    w = f64(np.asarray(w, np.float32).astype(ml_dtypes.bfloat16)).reshape(k // 32, 32, n)
    amax = np.abs(w).max(1)
    if fmt == "e4m3":
        byte = np.frexp(amax)[1] - 1 + 127 - 7
    else:
        mant, ex = np.frexp(amax / 6.0)
        byte = np.where(mant > 0.5, ex, ex - 1) + 127
    byte = np.clip(np.where(amax > 0, byte, 1), 1, 254)
    scaled = (w * np.exp2(127.0 - byte)[:, None, :]).reshape(k, n).astype(np.float32)
    by_word = np.ascontiguousarray(scaled.reshape(k // 512, 128, 4, n).transpose(0, 1, 3, 2))
    if fmt == "e4m3":
        words = by_word.astype(ml_dtypes.float8_e4m3fn).view(np.uint8)
    else:
        c = by_word.astype(ml_dtypes.float4_e2m1fn).view(np.uint8) & 0xF
        words = (c[..., 0::2] | (c[..., 1::2] << 4)).reshape(k // 512, 128, 2 * n)
    return np.ascontiguousarray(words), np.ascontiguousarray(byte.astype(np.uint8).reshape(k // 512, 16, n))


def unpack_weight(words, scales, fmt):
    g, _, n = scales.shape
    words = np.ascontiguousarray(words).reshape(g, 128, n, -1)
    if fmt == "e4m3":
        vals = words.view(ml_dtypes.float8_e4m3fn).astype(np.float64)
    else:
        nib = np.empty((g, 128, n, 4), np.uint8)
        nib[..., 0::2] = words & 0xF
        nib[..., 1::2] = words >> 4
        vals = E2M1[nib]
    vals = vals * np.repeat(np.exp2(scales.astype(np.float64) - 127.0), 8, axis=1)[..., None]
    return vals.transpose(0, 1, 3, 2).reshape(g * 512, n)


D, T, U, I, J, G = 512, 1024, 1024, 256, 512, 64


def setup_inputs():
    n = np.random.standard_normal
    idx = np.random.permutation(T)[:I]
    idx2 = np.random.permutation(U)[:J]
    fd = mx_kscale(D)
    tabbp = pack_weight(n((D, U)) / fd[:, None], "e2m1")
    return {
        "taba": (n((D, T)) * 1 / np.sqrt(D) * fd[:, None]).astype(np.float32),
        "dtab": (n((D, T)) * 1.3 / np.sqrt(D) * fd[:, None]).astype(np.float32),
        "tabb_words": tabbp[0],
        "tabb_scales": tabbp[1],
        "gw": (np.random.uniform(0.5, 2.0, (I, G))).astype(np.float32),
        "base": (0.3 * n((I, J))).astype(np.float32),
        "offs": striped(idx),
        "offs2": striped(idx2),
    }


def reference(taba, dtab, tabb_words, tabb_scales, gw, base, offs, offs2):
    idx = unstriped(offs)
    idx2 = unstriped(offs2)
    tabbu = unpack_weight(tabb_words, tabb_scales, "e2m1")
    tabaidxq = mxq(f64(taba)[:, idx], 0, "e4m3")
    tabbidx2g = tabbu[:, idx2]
    s = tabaidxq.T @ tabbidx2g
    dtabidxq = mxq(f64(dtab)[:, idx], 0, "e4m3")
    ts = dtabidxq.T @ tabbidx2g
    b = s - np.max(s, axis=1, keepdims=True)
    p = np.exp(b)
    z = np.sum(p, axis=1, keepdims=True)
    s1g = p.reshape(I, G, J // G).sum(axis=2)
    ds1g = f64(gw) / (s1g / z + 0.002) / z
    r1 = np.repeat(ds1g, J // G, axis=1)
    dz = np.sum(f64(gw) / (s1g / z + 0.002) * s1g / np.square(z) * (-1.0), axis=1, keepdims=True)
    dp = r1 + dz
    xb = ts
    xp = xb * p
    xz = np.sum(xp, axis=1, keepdims=True)
    xs1g = xp.reshape(I, G, J // G).sum(axis=2)
    xds1g = ((xs1g - xz * s1g / z) / z * f64(gw) / np.square(s1g / z + 0.002) * (-1.0) - xz * f64(gw) / (s1g / z + 0.002) / z) / z
    xr1 = np.repeat(xds1g, J // G, axis=1)
    xdz = np.sum(((xs1g - xz * s1g / z) / z * f64(gw) / np.square(s1g / z + 0.002) * (-1.0) * s1g + xs1g * f64(gw) / (s1g / z + 0.002) - xz * z * 2.0 * f64(gw) / (s1g / z + 0.002) * s1g / np.square(z)) / np.square(z) * (-1.0), axis=1, keepdims=True)
    xdp = xr1 + xdz
    xdb = xdp * p + xp * dp
    y = xdb * 4.0 + f64(base)
    return y

@@ -1,0 +1,268 @@
+from contextlib import ExitStack
+
+import concourse.mybir as mybir
+from concourse.masks import make_identity
+
+D, T, U, I, J, G = 512, 1024, 1024, 256, 512, 64
+FLOPS = 2 * 2 * D * I * J
+
+F32 = mybir.dt.float32
+BF16 = mybir.dt.bfloat16
+I32 = mybir.dt.int32
+U32 = mybir.dt.uint32
+U16 = mybir.dt.uint16
+U8 = mybir.dt.uint8
+FP8X4 = mybir.dt.float8_e4m3fn_x4
+FP4X4 = mybir.dt.float4_e2m1fn_x4
+ALU = mybir.AluOpType
+ACT = mybir.ActivationFunctionType
+AX = mybir.AxisListType
+
+P = 128
+PACK = 4
+R = J // G
+ROW_TILES = I // P
+EPS = 0.002
+GAIN = 4.0
+C, H = 4, 2
+
+
+def tile_attend_hvgrouplogshare_kernel(tc, taba, dtab, tabb_words, tabb_scales, gw, base, offs, offs2, out):
+    nc = tc.nc
+    with ExitStack() as ctx:
+        sb = ctx.enter_context(tc.tile_pool(name="sb", bufs=1))
+        ps = ctx.enter_context(tc.psum_pool(name="ps", bufs=1))
+
+        def tile(name, shape, dtype=F32, tag=None):
+            return sb.tile(shape, dtype, name=name, tag=tag or name, align_bytes=64)
+
+        list_b = tile("list_b", [P, J // 16], U16)
+        list_a = tile("list_a", [P, I // 16], U16)
+        words = tile("words", [P, U], U16)
+        scale_rows = tile("scale_rows", [P, U], U8)
+        ident = tile("ident", [P, P])
+
+        nc.gpsimd.memset(scale_rows[:].bitcast(I32), 0)
+        nc.sync.dma_start(list_b[:], offs2)
+        nc.sync.dma_start(out=words[:].bitcast(I32), in_=tabb_words[0].bitcast(I32))
+        for r in range(4):
+            nc.sync.dma_start(out=scale_rows[:].bitcast(I32)[r:P:32, :], in_=tabb_scales[0].bitcast(I32)[r:16:4, :])
+        nc.sync.dma_start(list_a[:], offs)
+
+        planes = {}
+        for name, table in (("a", taba), ("d", dtab)):
+            rows = table.rearrange("(p t) c -> p t c", t=PACK)
+            for t in range(PACK):
+                planes[name, t] = tile("plane_%s%d" % (name, t), [P, T])
+                nc.sync.dma_start(out=planes[name, t][:], in_=rows[:, t, :])
+            if name == "a":
+                gw_sb = tile("gw_sb", [P, ROW_TILES, G])
+                nc.sync.dma_start(out=gw_sb[:], in_=gw.rearrange("(r p) g -> p r g", p=P))
+        base_sb = []
+        for rt in range(ROW_TILES):
+            base_sb.append(tile("base%d" % rt, [P, J]))
+            nc.sync.dma_start(out=base_sb[rt][:], in_=base[rt * P : (rt + 1) * P, :])
+        make_identity(nc, ident[:])
+
+        listed_words = tile("listed_words", [P, J], U16)
+        b_words = tile("b_words", [P, J], U16)
+        b_scales = tile("b_scales", [P, J], U8)
+        nc.vector.tensor_copy(listed_words[:], words[:].indirect(list_b[:]))
+        nc.vector.tensor_copy(
+            b_scales[:].rearrange("p (c g h) -> p g c h", c=C, h=H), scale_rows[:].indirect(list_b[:])
+        )
+        nc.vector.tensor_copy(
+            out=b_words[:].rearrange("p (c g h) -> p c g h", c=C, h=H),
+            in_=listed_words[:].rearrange("p (g c h) -> p c g h", c=C, h=H),
+        )
+
+        def listed(name, t, lo=0, hi=I):
+            return planes[name, t][:].indirect(list_a[:, lo // 16 : hi // 16])
+
+        def weave(woven, picked, u, rt):
+            nc.vector.tensor_copy(
+                out=woven[:, :, 2 * u : 2 * u + 2], in_=picked[:, :, rt * P : (rt + 1) * P].rearrange("p t i -> p i t")
+            )
+
+        def quantise(name, woven):
+            codes = tile("codes_" + name, [P, P], U32)
+            scales = tile("scales_" + name, [P, P], U8)
+            nc.vector.quantize_mx(
+                out=codes[:].bitcast(FP8X4), scales=scales[:], in_=woven[:].rearrange("p i t -> p (i t)")
+            )
+            return codes, scales
+
+        def turn(dst, src, start, stop):
+            nc.tensor.matmul(dst, lhsT=src, rhs=ident[:], is_transpose=True, start=start, stop=stop)
+
+        def chunk(ap, c):
+            return ap[:, c * P : (c + 1) * P]
+
+        def twice(ap):
+            return ap.unsqueeze(2).to_broadcast([P, G, H])
+
+        def over_chunks(ap):
+            return ap.unsqueeze(1).to_broadcast([P, C, P])
+
+        def by_chunk(ap):
+            return ap.rearrange("p (c i) -> p c i", c=C)
+
+        rows = [dict() for rt in range(ROW_TILES)]
+
+        a_low = tile("a_low", [P, 2, I], BF16)
+        a_high = tile("a_high", [P, 2, I], BF16)
+        nc.scalar.activation(a_low[:, 0, :], listed("a", 0), ACT.Copy)
+        nc.vector.tensor_copy(a_low[:, 1, :], listed("a", 1))
+        nc.scalar.activation(a_high[:, 0, :], listed("a", 2), ACT.Copy)
+        for rt, f in enumerate(rows):
+            f["woven_a"] = tile("woven_a%d" % rt, [P, P, PACK], BF16)
+            weave(f["woven_a"], a_low, 0, rt)
+        nc.vector.tensor_copy(a_high[:, 1, 0:P], listed("a", 3, 0, P))
+        nc.scalar.activation(a_high[:, 1, P:I], listed("a", 3, P, I), ACT.Copy)
+        for rt, f in enumerate(rows):
+            weave(f["woven_a"], a_high, 1, rt)
+        for rt, f in enumerate(rows):
+            scaled_gw = tile("scaled_gw%d" % rt, [P, G])
+            f["gw_sum"] = tile("gw_sum%d" % rt, [P, 1])
+            nc.scalar.activation(
+                out=scaled_gw[:], in_=gw_sb[:, rt, :], func=ACT.Copy, scale=GAIN / EPS, accum_out=f["gw_sum"][:]
+            )
+        d_low = tile("d_low", [P, 2, I], BF16)
+        for rt, f in enumerate(rows):
+            codes, scales = quantise("a%d" % rt, f["woven_a"])
+            f["s"] = ps.tile([P, J], F32, name="s%d" % rt, tag="wide%d" % rt)
+            nc.tensor.matmul_mx(
+                out=f["s"][:], lhsT=codes[:].bitcast(FP8X4), lhsT_scale=scales[:],
+                rhs=b_words[:].bitcast(FP4X4), rhs_scale=b_scales[:], start=True, stop=True,
+            )
+        for t in range(2):
+            nc.scalar.activation(d_low[:, t, :], listed("d", t), ACT.Copy)
+        for rt, f in enumerate(rows):
+            neg_max = tile("neg_max%d" % rt, [P, 1])[:]
+            nc.vector.tensor_reduce(out=neg_max, in_=f["s"][:], axis=AX.X, op=ALU.max, negate=True)
+            f["p"] = tile("p%d" % rt, [P, J], tag=("plane_d1", "p1")[rt])
+            f["den"] = tile("den%d" % rt, [P, G + 1])
+            nc.scalar.activation(
+                out=f["p"][:], in_=f["s"][:], func=ACT.Exp, bias=neg_max, accum_out=f["den"][:, G : G + 1]
+            )
+            f["p_turned"] = ps.tile([P, J], F32, name="p_turned%d" % rt, tag="mid%d" % rt)
+            for c in range(C):
+                turn(chunk(f["p_turned"], c), chunk(f["p"], c), True, True)
+        for rt, f in enumerate(rows):
+            f["woven_d"] = tile("woven_d%d" % rt, [P, P, PACK], BF16)
+            weave(f["woven_d"], d_low, 0, rt)
+        d_high = tile("d_high", [P, 2, I], BF16, tag="neg_max0")
+        nc.vector.tensor_copy(d_high[:, 0, :], listed("d", 2))
+        nc.scalar.activation(d_high[:, 1, :], listed("d", 3), ACT.Copy)
+        for rt, f in enumerate(rows):
+            weave(f["woven_d"], d_high, 1, rt)
+        both_pT = tile("pT", [P, ROW_TILES, J], tag="plane_d3")
+        for rt, f in enumerate(rows):
+            f["pT"] = both_pT[:, rt, :]
+            nc.scalar.copy(out=f["pT"], in_=f["p_turned"][:])
+        for rt, f in enumerate(rows):
+            codes, scales = quantise("d%d" % rt, f["woven_d"])
+            f["ts"] = ps.tile([P, J], F32, name="ts%d" % rt)
+            for c in range(C):
+                nc.tensor.matmul_mx(
+                    out=chunk(f["ts"], c), lhsT=chunk(b_words, c).bitcast(FP4X4), lhsT_scale=chunk(b_scales, c),
+                    rhs=codes[:].bitcast(FP8X4), rhs_scale=scales[:], start=True, stop=True,
+                )
+        for rt, f in enumerate(rows):
+            f["neg_s1"] = tile("neg_s1_%d" % rt, [P, G], tag=("neg_s1_0", "neg_max0")[rt])[:]
+            nc.vector.tensor_reduce(
+                out=f["neg_s1"], in_=f["p"][:].rearrange("p (c g h) -> p g c h", c=C, h=H),
+                axis=AX.XY, op=ALU.add, negate=True,
+            )
+            nc.vector.scalar_tensor_tensor(
+                out=f["den"][:, 0:G], in0=f["den"][:, G : G + 1].to_broadcast([P, G]), scalar=EPS,
+                in1=f["neg_s1"], op0=ALU.mult, op1=ALU.subtract,
+            )
+        for rt, f in enumerate(rows):
+            root = tile("root%d" % rt, [P, G + 1], tag="woven_d%d" % rt)[:]
+            nc.scalar.activation(out=root, in_=f["den"][:], func=ACT.Abs_reciprocal_sqrt)
+            f["inv"] = tile("inv%d" % rt, [P, G + 1])
+            nc.scalar.activation(out=f["inv"][:], in_=root, func=ACT.Square)
+        for rt, f in enumerate(rows):
+            f["xpT"] = tile("xpT%d" % rt, [P, J])
+            nc.vector.tensor_tensor(out=f["xpT"][:], in0=f["ts"][:], in1=f["pT"], op=ALU.mult)
+            f["pairs"] = ps.tile([P, P], F32, name="pairs%d" % rt, tag="mid%d" % rt)
+            for c in range(C):
+                turn(f["pairs"][:], chunk(f["xpT"], c), c == 0, c == C - 1)
+        for rt, f in enumerate(rows):
+            scaled_pairs = tile("scaled_pairs%d" % rt, [P, P])
+            f["xz_eps"] = tile("xz_eps%d" % rt, [P, 1])
+            nc.scalar.activation(
+                out=scaled_pairs[:], in_=f["pairs"][:], func=ACT.Copy, scale=EPS, accum_out=f["xz_eps"][:]
+            )
+            f["xz_gw"] = tile("xz_gw%d" % rt, [P, 1])
+            nc.scalar.activation(out=f["xz_gw"][:], in_=f["xz_eps"][:], func=ACT.Copy, scale=f["gw_sum"][:])
+        for rt, f in enumerate(rows):
+            f["w"] = tile("w%d" % rt, [P, G, H], tag=("codes_d1", "scales_d1")[rt])
+            nc.vector.scalar_tensor_tensor(
+                out=f["w"][:], in0=twice(gw_sb[:, rt, :]), scalar=GAIN, in1=twice(f["inv"][:, 0:G]),
+                op0=ALU.mult, op1=ALU.mult,
+            )
+        for rt, f in enumerate(rows):
+            f["curv"] = tile("curv%d" % rt, [P, G])
+            nc.vector.scalar_tensor_tensor(
+                out=f["curv"][:], in0=f["w"][:, :, 0], scalar=-1.0, in1=f["inv"][:, 0:G], op0=ALU.mult, op1=ALU.mult
+            )
+            terms = tile("mean_terms%d" % rt, [P, G])
+            neg_mean = tile("neg_mean%d" % rt, [P, 1])
+            nc.vector.scalar_tensor_tensor(
+                out=terms[:], in0=f["w"][:, :, 0], scalar=f["inv"][:, G : G + 1], in1=f["neg_s1"],
+                op0=ALU.mult, op1=ALU.mult, accum_out=neg_mean[:],
+            )
+            f["bT"] = ps.tile([P, P], F32, name="bT%d" % rt)
+            turn(f["bT"][:], f["w"][:].rearrange("p g h -> p (g h)"), True, False)
+            turn(f["bT"][:], neg_mean[:].to_broadcast([P, P]), False, True)
+        for rt, f in enumerate(rows):
+            f["first"] = tile("first%d" % rt, [P, J])
+            f["xs1"] = f["first"][:, 0:G]
+            nc.vector.tensor_reduce(
+                out=f["xs1"], in_=f["pairs"][:].rearrange("p (g h) -> p g h", h=H), axis=AX.X, op=ALU.add
+            )
+        for rt, f in enumerate(rows):
+            inv_z = f["inv"][:, G : G + 1]
+            f["xz_k"] = tile("xz_k%d" % rt, [P, 1])
+            nc.vector.tensor_scalar(
+                out=f["xz_k"][:], in0=f["xz_gw"][:], scalar1=inv_z, scalar2=inv_z, op0=ALU.mult, op1=ALU.mult
+            )
+            f["y"] = tile("y%d" % rt, [P, G, H])
+            f["y_sum"] = tile("y_sum%d" % rt, [P, 1])
+            nc.vector.scalar_tensor_tensor(
+                out=f["y"][:], in0=twice(f["xs1"]), scalar=f["xz_eps"][:], in1=twice(f["curv"][:]),
+                op0=ALU.add, op1=ALU.mult, accum_out=f["y_sum"][:],
+            )
+        for rt, f in enumerate(rows):
+            shift = tile("shift%d" % rt, [P, 1])
+            nc.vector.tensor_scalar(
+                out=shift[:], in0=f["y_sum"][:], scalar1=EPS / H, scalar2=f["xz_k"][:], op0=ALU.mult, op1=ALU.add
+            )
+            f["dT"] = ps.tile([P, P], F32, name="dT%d" % rt, tag="mid%d" % rt)
+            turn(f["dT"][:], f["y"][:].rearrange("p g h -> p (g h)"), True, False)
+            turn(f["dT"][:], shift[:].to_broadcast([P, P]), False, True)
+        for rt, f in enumerate(rows):
+            first = f["first"]
+            nc.vector.tensor_tensor(
+                out=by_chunk(first[:]), in0=over_chunks(f["bT"][:]), in1=by_chunk(f["xpT"][:]), op=ALU.mult
+            )
+            f["total"] = ps.tile([P, J], F32, name="total%d" % rt, tag="wide%d" % rt)
+            for c in range(C):
+                turn(chunk(f["total"], c), chunk(first, c), c == 0, False)
+            second = tile("second%d" % rt, [P, J])
+            nc.vector.tensor_tensor(
+                out=by_chunk(second[:]), in0=over_chunks(f["dT"][:]), in1=by_chunk(f["pT"]), op=ALU.mult
+            )
+            for c in range(C):
+                turn(chunk(f["total"], c), chunk(second, c), False, c == C - 1)
+        for rt, f in enumerate(rows):
+            result = tile("result%d" % rt, [P, J])
+            nc.vector.tensor_tensor(
+                out=result[:].rearrange("p (g c h) -> p g c h", c=C, h=H),
+                in0=f["total"][:].rearrange("p (c g h) -> p g c h", c=C, h=H),
+                in1=base_sb[rt][:].rearrange("p (g c h) -> p g c h", c=C, h=H),
+                op=ALU.add,
+            )
+            nc.sync.dma_start(out=out[rt * P : (rt + 1) * P, :], in_=result[:])

@@ -43,10 +43,12 @@ def tile_attend_hvgrouplogshare_kernel(tc, taba, dtab, tabb_words, tabb_scales, 
         ident = tile("ident", [P, P])
 
         nc.gpsimd.memset(scale_rows[:].bitcast(I32), 0)
+        for r in range(4):
+            nc.gpsimd.dma_start(out=scale_rows[:].bitcast(I32)[r:P:32, :], in_=tabb_scales[0].bitcast(I32)[r:16:4, :])
         nc.sync.dma_start(list_b[:], offs2)
         nc.sync.dma_start(out=words[:].bitcast(I32), in_=tabb_words[0].bitcast(I32))
-        for r in range(4):
-            nc.sync.dma_start(out=scale_rows[:].bitcast(I32)[r:P:32, :], in_=tabb_scales[0].bitcast(I32)[r:16:4, :])
+        gw_sb = tile("gw_sb", [P, ROW_TILES, G])
+        nc.sync.dma_start(out=gw_sb[:], in_=gw.rearrange("(r p) g -> p r g", p=P))
         nc.sync.dma_start(list_a[:], offs)
 
         planes = {}
@@ -55,9 +57,6 @@ def tile_attend_hvgrouplogshare_kernel(tc, taba, dtab, tabb_words, tabb_scales, 
             for t in range(PACK):
                 planes[name, t] = tile("plane_%s%d" % (name, t), [P, T])
                 nc.sync.dma_start(out=planes[name, t][:], in_=rows[:, t, :])
-            if name == "a":
-                gw_sb = tile("gw_sb", [P, ROW_TILES, G])
-                nc.sync.dma_start(out=gw_sb[:], in_=gw.rearrange("(r p) g -> p r g", p=P))
         base_sb = []
         for rt in range(ROW_TILES):
             base_sb.append(tile("base%d" % rt, [P, J]))
@@ -109,10 +108,16 @@ def tile_attend_hvgrouplogshare_kernel(tc, taba, dtab, tabb_words, tabb_scales, 
 
         rows = [dict() for rt in range(ROW_TILES)]
 
+        for rt, f in enumerate(rows):
+            f["gain_gw"] = tile("gain_gw%d" % rt, [P, G])
+            f["gw_sum"] = tile("gw_sum%d" % rt, [P, 1])
+            nc.scalar.activation(
+                out=f["gain_gw"][:], in_=gw_sb[:, rt, :], func=ACT.Copy, scale=GAIN, accum_out=f["gw_sum"][:]
+            )
         a_low = tile("a_low", [P, 2, I], BF16)
         a_high = tile("a_high", [P, 2, I], BF16)
         nc.scalar.activation(a_low[:, 0, :], listed("a", 0), ACT.Copy)
-        nc.vector.tensor_copy(a_low[:, 1, :], listed("a", 1))
+        nc.scalar.activation(a_low[:, 1, :], listed("a", 1), ACT.Copy)
         nc.scalar.activation(a_high[:, 0, :], listed("a", 2), ACT.Copy)
         for rt, f in enumerate(rows):
             f["woven_a"] = tile("woven_a%d" % rt, [P, P, PACK], BF16)
@@ -121,12 +126,6 @@ def tile_attend_hvgrouplogshare_kernel(tc, taba, dtab, tabb_words, tabb_scales, 
         nc.scalar.activation(a_high[:, 1, P:I], listed("a", 3, P, I), ACT.Copy)
         for rt, f in enumerate(rows):
             weave(f["woven_a"], a_high, 1, rt)
-        for rt, f in enumerate(rows):
-            scaled_gw = tile("scaled_gw%d" % rt, [P, G])
-            f["gw_sum"] = tile("gw_sum%d" % rt, [P, 1])
-            nc.scalar.activation(
-                out=scaled_gw[:], in_=gw_sb[:, rt, :], func=ACT.Copy, scale=GAIN / EPS, accum_out=f["gw_sum"][:]
-            )
         d_low = tile("d_low", [P, 2, I], BF16)
         for rt, f in enumerate(rows):
             codes, scales = quantise("a%d" % rt, f["woven_a"])
@@ -179,35 +178,32 @@ def tile_attend_hvgrouplogshare_kernel(tc, taba, dtab, tabb_words, tabb_scales, 
                 in1=f["neg_s1"], op0=ALU.mult, op1=ALU.subtract,
             )
         for rt, f in enumerate(rows):
-            root = tile("root%d" % rt, [P, G + 1], tag="woven_d%d" % rt)[:]
-            nc.scalar.activation(out=root, in_=f["den"][:], func=ACT.Abs_reciprocal_sqrt)
-            f["inv"] = tile("inv%d" % rt, [P, G + 1])
-            nc.scalar.activation(out=f["inv"][:], in_=root, func=ACT.Square)
-        for rt, f in enumerate(rows):
             f["xpT"] = tile("xpT%d" % rt, [P, J])
             nc.vector.tensor_tensor(out=f["xpT"][:], in0=f["ts"][:], in1=f["pT"], op=ALU.mult)
             f["pairs"] = ps.tile([P, P], F32, name="pairs%d" % rt, tag="mid%d" % rt)
             for c in range(C):
                 turn(f["pairs"][:], chunk(f["xpT"], c), c == 0, c == C - 1)
         for rt, f in enumerate(rows):
-            scaled_pairs = tile("scaled_pairs%d" % rt, [P, P])
-            f["xz_eps"] = tile("xz_eps%d" % rt, [P, 1])
+            f["pair_sums"] = tile("pair_sums%d" % rt, [P, G, H])
+            xz = tile("xz%d" % rt, [P, 1])
             nc.scalar.activation(
-                out=scaled_pairs[:], in_=f["pairs"][:], func=ACT.Copy, scale=EPS, accum_out=f["xz_eps"][:]
+                out=f["pair_sums"][:].rearrange("p g h -> p (g h)"), in_=f["pairs"][:], func=ACT.Copy, accum_out=xz[:]
             )
+            f["xz_eps"] = tile("xz_eps%d" % rt, [P, 1])
+            nc.scalar.activation(out=f["xz_eps"][:], in_=xz[:], func=ACT.Copy, scale=EPS)
             f["xz_gw"] = tile("xz_gw%d" % rt, [P, 1])
-            nc.scalar.activation(out=f["xz_gw"][:], in_=f["xz_eps"][:], func=ACT.Copy, scale=f["gw_sum"][:])
+            nc.scalar.activation(out=f["xz_gw"][:], in_=xz[:], func=ACT.Copy, scale=f["gw_sum"][:])
         for rt, f in enumerate(rows):
-            f["w"] = tile("w%d" % rt, [P, G, H], tag=("codes_d1", "scales_d1")[rt])
-            nc.vector.scalar_tensor_tensor(
-                out=f["w"][:], in0=twice(gw_sb[:, rt, :]), scalar=GAIN, in1=twice(f["inv"][:, 0:G]),
-                op0=ALU.mult, op1=ALU.mult,
+            f["inv"] = tile("inv%d" % rt, [P, G + 1], tag=("codes_d1", "scales_d1")[rt])
+            nc.vector.reciprocal(out=f["inv"][:], in_=f["den"][:])
+        for rt, f in enumerate(rows):
+            f["w"] = tile("w%d" % rt, [P, G, H])
+            nc.vector.tensor_tensor(
+                out=f["w"][:], in0=twice(f["gain_gw"][:]), in1=twice(f["inv"][:, 0:G]), op=ALU.mult
             )
         for rt, f in enumerate(rows):
             f["curv"] = tile("curv%d" % rt, [P, G])
-            nc.vector.scalar_tensor_tensor(
-                out=f["curv"][:], in0=f["w"][:, :, 0], scalar=-1.0, in1=f["inv"][:, 0:G], op0=ALU.mult, op1=ALU.mult
-            )
+            nc.vector.tensor_tensor(out=f["curv"][:], in0=f["w"][:, :, 0], in1=f["inv"][:, 0:G], op=ALU.mult)
             terms = tile("mean_terms%d" % rt, [P, G])
             neg_mean = tile("neg_mean%d" % rt, [P, 1])
             nc.vector.scalar_tensor_tensor(
@@ -219,9 +215,10 @@ def tile_attend_hvgrouplogshare_kernel(tc, taba, dtab, tabb_words, tabb_scales, 
             turn(f["bT"][:], neg_mean[:].to_broadcast([P, P]), False, True)
         for rt, f in enumerate(rows):
             f["first"] = tile("first%d" % rt, [P, J])
-            f["xs1"] = f["first"][:, 0:G]
-            nc.vector.tensor_reduce(
-                out=f["xs1"], in_=f["pairs"][:].rearrange("p (g h) -> p g h", h=H), axis=AX.X, op=ALU.add
+            f["x_den"] = f["first"][:, 0:G]
+            nc.vector.scalar_tensor_tensor(
+                out=f["x_den"], in0=f["pair_sums"][:, :, 0], scalar=f["xz_eps"][:], in1=f["pair_sums"][:, :, 1],
+                op0=ALU.add, op1=ALU.add,
             )
         for rt, f in enumerate(rows):
             inv_z = f["inv"][:, G : G + 1]
@@ -232,8 +229,8 @@ def tile_attend_hvgrouplogshare_kernel(tc, taba, dtab, tabb_words, tabb_scales, 
             f["y"] = tile("y%d" % rt, [P, G, H])
             f["y_sum"] = tile("y_sum%d" % rt, [P, 1])
             nc.vector.scalar_tensor_tensor(
-                out=f["y"][:], in0=twice(f["xs1"]), scalar=f["xz_eps"][:], in1=twice(f["curv"][:]),
-                op0=ALU.add, op1=ALU.mult, accum_out=f["y_sum"][:],
+                out=f["y"][:], in0=twice(f["x_den"]), scalar=-1.0, in1=twice(f["curv"][:]),
+                op0=ALU.mult, op1=ALU.mult, accum_out=f["y_sum"][:],
             )
         for rt, f in enumerate(rows):
             shift = tile("shift%d" % rt, [P, 1])
@@ -258,11 +255,14 @@ def tile_attend_hvgrouplogshare_kernel(tc, taba, dtab, tabb_words, tabb_scales, 
             for c in range(C):
                 turn(chunk(f["total"], c), chunk(second, c), False, c == C - 1)
         for rt, f in enumerate(rows):
-            result = tile("result%d" % rt, [P, J])
-            nc.vector.tensor_tensor(
-                out=result[:].rearrange("p (g c h) -> p g c h", c=C, h=H),
-                in0=f["total"][:].rearrange("p (c g h) -> p g c h", c=C, h=H),
-                in1=base_sb[rt][:].rearrange("p (g c h) -> p g c h", c=C, h=H),
-                op=ALU.add,
-            )
-            nc.sync.dma_start(out=out[rt * P : (rt + 1) * P, :], in_=result[:])
+            for half, queue in enumerate((nc.sync, nc.scalar)):
+                groups = slice(half * G // 2, (half + 1) * G // 2)
+                cols = slice(half * J // 2, (half + 1) * J // 2)
+                result = tile("result%d_%d" % (rt, half), [P, J // 2])
+                nc.vector.tensor_tensor(
+                    out=result[:].rearrange("p (g c h) -> p g c h", c=C, h=H),
+                    in0=f["total"][:].rearrange("p (c g h) -> p g c h", c=C, h=H)[:, groups],
+                    in1=base_sb[rt][:, cols].rearrange("p (g c h) -> p g c h", c=C, h=H),
+                    op=ALU.add,
+                )
+                queue.dma_start(out=out[rt * P : (rt + 1) * P, cols], in_=result[:])

@@ -43,12 +43,10 @@ def tile_attend_hvgrouplogshare_kernel(tc, taba, dtab, tabb_words, tabb_scales, 
         ident = tile("ident", [P, P])
 
         nc.gpsimd.memset(scale_rows[:].bitcast(I32), 0)
-        for r in range(4):
-            nc.gpsimd.dma_start(out=scale_rows[:].bitcast(I32)[r:P:32, :], in_=tabb_scales[0].bitcast(I32)[r:16:4, :])
         nc.sync.dma_start(list_b[:], offs2)
         nc.sync.dma_start(out=words[:].bitcast(I32), in_=tabb_words[0].bitcast(I32))
-        gw_sb = tile("gw_sb", [P, ROW_TILES, G])
-        nc.sync.dma_start(out=gw_sb[:], in_=gw.rearrange("(r p) g -> p r g", p=P))
+        for r in range(4):
+            nc.sync.dma_start(out=scale_rows[:].bitcast(I32)[r:P:32, :], in_=tabb_scales[0].bitcast(I32)[r:16:4, :])
         nc.sync.dma_start(list_a[:], offs)
 
         planes = {}
@@ -57,6 +55,9 @@ def tile_attend_hvgrouplogshare_kernel(tc, taba, dtab, tabb_words, tabb_scales, 
             for t in range(PACK):
                 planes[name, t] = tile("plane_%s%d" % (name, t), [P, T])
                 nc.sync.dma_start(out=planes[name, t][:], in_=rows[:, t, :])
+            if name == "a":
+                gw_sb = tile("gw_sb", [P, ROW_TILES, G])
+                nc.sync.dma_start(out=gw_sb[:], in_=gw.rearrange("(r p) g -> p r g", p=P))
         base_sb = []
         for rt in range(ROW_TILES):
             base_sb.append(tile("base%d" % rt, [P, J]))
@@ -78,10 +79,13 @@ def tile_attend_hvgrouplogshare_kernel(tc, taba, dtab, tabb_words, tabb_scales, 
         def listed(name, t, lo=0, hi=I):
             return planes[name, t][:].indirect(list_a[:, lo // 16 : hi // 16])
 
-        def weave(woven, picked, u, rt):
+        def weave(name, picked, rt):
+            woven = tile("woven_%s%d" % (name, rt), [P, P, PACK], BF16)
             nc.vector.tensor_copy(
-                out=woven[:, :, 2 * u : 2 * u + 2], in_=picked[:, :, rt * P : (rt + 1) * P].rearrange("p t i -> p i t")
+                out=woven[:].rearrange("p (c i) t -> p c t i", i=4),
+                in_=picked[:, :, rt * P : (rt + 1) * P].rearrange("p t (c i) -> p c t i", i=4),
             )
+            return woven
 
         def quantise(name, woven):
             codes = tile("codes_" + name, [P, P], U32)
@@ -108,25 +112,21 @@ def tile_attend_hvgrouplogshare_kernel(tc, taba, dtab, tabb_words, tabb_scales, 
 
         rows = [dict() for rt in range(ROW_TILES)]
 
+        picked_a = tile("picked_a", [P, PACK, I], BF16)
+        nc.scalar.activation(picked_a[:, 0, :], listed("a", 0), ACT.Copy)
+        nc.vector.tensor_copy(picked_a[:, 1, :], listed("a", 1))
+        nc.scalar.activation(picked_a[:, 2, :], listed("a", 2), ACT.Copy)
+        nc.vector.tensor_copy(picked_a[:, 3, 0:P], listed("a", 3, 0, P))
+        nc.scalar.activation(picked_a[:, 3, P:I], listed("a", 3, P, I), ACT.Copy)
+        for rt, f in enumerate(rows):
+            f["woven_a"] = weave("a", picked_a, rt)
         for rt, f in enumerate(rows):
             f["gain_gw"] = tile("gain_gw%d" % rt, [P, G])
             f["gw_sum"] = tile("gw_sum%d" % rt, [P, 1])
             nc.scalar.activation(
                 out=f["gain_gw"][:], in_=gw_sb[:, rt, :], func=ACT.Copy, scale=GAIN, accum_out=f["gw_sum"][:]
             )
-        a_low = tile("a_low", [P, 2, I], BF16)
-        a_high = tile("a_high", [P, 2, I], BF16)
-        nc.scalar.activation(a_low[:, 0, :], listed("a", 0), ACT.Copy)
-        nc.scalar.activation(a_low[:, 1, :], listed("a", 1), ACT.Copy)
-        nc.scalar.activation(a_high[:, 0, :], listed("a", 2), ACT.Copy)
-        for rt, f in enumerate(rows):
-            f["woven_a"] = tile("woven_a%d" % rt, [P, P, PACK], BF16)
-            weave(f["woven_a"], a_low, 0, rt)
-        nc.vector.tensor_copy(a_high[:, 1, 0:P], listed("a", 3, 0, P))
-        nc.scalar.activation(a_high[:, 1, P:I], listed("a", 3, P, I), ACT.Copy)
-        for rt, f in enumerate(rows):
-            weave(f["woven_a"], a_high, 1, rt)
-        d_low = tile("d_low", [P, 2, I], BF16)
+        picked_d = tile("picked_d", [P, PACK, I], BF16)
         for rt, f in enumerate(rows):
             codes, scales = quantise("a%d" % rt, f["woven_a"])
             f["s"] = ps.tile([P, J], F32, name="s%d" % rt, tag="wide%d" % rt)
@@ -134,12 +134,12 @@ def tile_attend_hvgrouplogshare_kernel(tc, taba, dtab, tabb_words, tabb_scales, 
                 out=f["s"][:], lhsT=codes[:].bitcast(FP8X4), lhsT_scale=scales[:],
                 rhs=b_words[:].bitcast(FP4X4), rhs_scale=b_scales[:], start=True, stop=True,
             )
-        for t in range(2):
-            nc.scalar.activation(d_low[:, t, :], listed("d", t), ACT.Copy)
+        nc.scalar.activation(picked_d[:, 0, :], listed("d", 0), ACT.Copy)
         for rt, f in enumerate(rows):
+            nc.scalar.activation(picked_d[:, 1 + rt, :], listed("d", 1 + rt), ACT.Copy)
             neg_max = tile("neg_max%d" % rt, [P, 1])[:]
             nc.vector.tensor_reduce(out=neg_max, in_=f["s"][:], axis=AX.X, op=ALU.max, negate=True)
-            f["p"] = tile("p%d" % rt, [P, J], tag=("plane_d1", "p1")[rt])
+            f["p"] = tile("p%d" % rt, [P, J], tag="plane_d%d" % (1 + rt))
             f["den"] = tile("den%d" % rt, [P, G + 1])
             nc.scalar.activation(
                 out=f["p"][:], in_=f["s"][:], func=ACT.Exp, bias=neg_max, accum_out=f["den"][:, G : G + 1]
@@ -147,17 +147,11 @@ def tile_attend_hvgrouplogshare_kernel(tc, taba, dtab, tabb_words, tabb_scales, 
             f["p_turned"] = ps.tile([P, J], F32, name="p_turned%d" % rt, tag="mid%d" % rt)
             for c in range(C):
                 turn(chunk(f["p_turned"], c), chunk(f["p"], c), True, True)
+        nc.vector.tensor_copy(picked_d[:, 3, :], listed("d", 3))
         for rt, f in enumerate(rows):
-            f["woven_d"] = tile("woven_d%d" % rt, [P, P, PACK], BF16)
-            weave(f["woven_d"], d_low, 0, rt)
-        d_high = tile("d_high", [P, 2, I], BF16, tag="neg_max0")
-        nc.vector.tensor_copy(d_high[:, 0, :], listed("d", 2))
-        nc.scalar.activation(d_high[:, 1, :], listed("d", 3), ACT.Copy)
+            f["woven_d"] = weave("d", picked_d, rt)
         for rt, f in enumerate(rows):
-            weave(f["woven_d"], d_high, 1, rt)
-        both_pT = tile("pT", [P, ROW_TILES, J], tag="plane_d3")
-        for rt, f in enumerate(rows):
-            f["pT"] = both_pT[:, rt, :]
+            f["pT"] = tile("pT%d" % rt, [P, J])[:]
             nc.scalar.copy(out=f["pT"], in_=f["p_turned"][:])
         for rt, f in enumerate(rows):
             codes, scales = quantise("d%d" % rt, f["woven_d"])
@@ -168,7 +162,7 @@ def tile_attend_hvgrouplogshare_kernel(tc, taba, dtab, tabb_words, tabb_scales, 
                     rhs=codes[:].bitcast(FP8X4), rhs_scale=scales[:], start=True, stop=True,
                 )
         for rt, f in enumerate(rows):
-            f["neg_s1"] = tile("neg_s1_%d" % rt, [P, G], tag=("neg_s1_0", "neg_max0")[rt])[:]
+            f["neg_s1"] = tile("neg_s1_%d" % rt, [P, G], tag=("neg_s1_0", "picked_d")[rt])[:]
             nc.vector.tensor_reduce(
                 out=f["neg_s1"], in_=f["p"][:].rearrange("p (c g h) -> p g c h", c=C, h=H),
                 axis=AX.XY, op=ALU.add, negate=True,
@@ -177,6 +171,11 @@ def tile_attend_hvgrouplogshare_kernel(tc, taba, dtab, tabb_words, tabb_scales, 
                 out=f["den"][:, 0:G], in0=f["den"][:, G : G + 1].to_broadcast([P, G]), scalar=EPS,
                 in1=f["neg_s1"], op0=ALU.mult, op1=ALU.subtract,
             )
+        for rt, f in enumerate(rows):
+            root = tile("root%d" % rt, [P, G + 1], tag="codes_d%d" % rt)
+            nc.scalar.activation(out=root[:], in_=f["den"][:], func=ACT.Abs_reciprocal_sqrt)
+            f["inv"] = tile("inv%d" % rt, [P, G + 1])
+            nc.scalar.activation(out=f["inv"][:], in_=root[:], func=ACT.Square)
         for rt, f in enumerate(rows):
             f["xpT"] = tile("xpT%d" % rt, [P, J])
             nc.vector.tensor_tensor(out=f["xpT"][:], in0=f["ts"][:], in1=f["pT"], op=ALU.mult)
@@ -193,9 +192,6 @@ def tile_attend_hvgrouplogshare_kernel(tc, taba, dtab, tabb_words, tabb_scales, 
             nc.scalar.activation(out=f["xz_eps"][:], in_=xz[:], func=ACT.Copy, scale=EPS)
             f["xz_gw"] = tile("xz_gw%d" % rt, [P, 1])
             nc.scalar.activation(out=f["xz_gw"][:], in_=xz[:], func=ACT.Copy, scale=f["gw_sum"][:])
-        for rt, f in enumerate(rows):
-            f["inv"] = tile("inv%d" % rt, [P, G + 1], tag=("codes_d1", "scales_d1")[rt])
-            nc.vector.reciprocal(out=f["inv"][:], in_=f["den"][:])
         for rt, f in enumerate(rows):
             f["w"] = tile("w%d" % rt, [P, G, H])
             nc.vector.tensor_tensor(
@@ -248,12 +244,14 @@ def tile_attend_hvgrouplogshare_kernel(tc, taba, dtab, tabb_words, tabb_scales, 
             f["total"] = ps.tile([P, J], F32, name="total%d" % rt, tag="wide%d" % rt)
             for c in range(C):
                 turn(chunk(f["total"], c), chunk(first, c), c == 0, False)
-            second = tile("second%d" % rt, [P, J])
-            nc.vector.tensor_tensor(
-                out=by_chunk(second[:]), in0=over_chunks(f["dT"][:]), in1=by_chunk(f["pT"]), op=ALU.mult
-            )
-            for c in range(C):
-                turn(chunk(f["total"], c), chunk(second, c), False, c == C - 1)
+            for lo in range(0, C, C // 2):
+                second = tile("second%d_%d" % (rt, lo), [P, C // 2, P])
+                nc.vector.tensor_tensor(
+                    out=second[:], in0=over_chunks(f["dT"][:])[:, lo : lo + C // 2, :],
+                    in1=by_chunk(f["pT"])[:, lo : lo + C // 2, :], op=ALU.mult,
+                )
+                for c in range(lo, lo + C // 2):
+                    turn(chunk(f["total"], c), second[:, c - lo, :], False, c == C - 1)
         for rt, f in enumerate(rows):
             for half, queue in enumerate((nc.sync, nc.scalar)):
                 groups = slice(half * G // 2, (half + 1) * G // 2)

from contextlib import ExitStack

import concourse.mybir as mybir
from concourse.masks import make_identity

D, T, U, I, J, G = 512, 1024, 1024, 256, 512, 64
FLOPS = 2 * 2 * D * I * J

F32 = mybir.dt.float32
BF16 = mybir.dt.bfloat16
I32 = mybir.dt.int32
U32 = mybir.dt.uint32
U16 = mybir.dt.uint16
U8 = mybir.dt.uint8
FP8X4 = mybir.dt.float8_e4m3fn_x4
FP4X4 = mybir.dt.float4_e2m1fn_x4
ALU = mybir.AluOpType
ACT = mybir.ActivationFunctionType
AX = mybir.AxisListType

P = 128
PACK = 4
R = J // G
ROW_TILES = I // P
EPS = 0.002
GAIN = 4.0
C, H = 4, 2


def tile_attend_hvgrouplogshare_kernel(tc, taba, dtab, tabb_words, tabb_scales, gw, base, offs, offs2, out):
    nc = tc.nc
    with ExitStack() as ctx:
        sb = ctx.enter_context(tc.tile_pool(name="sb", bufs=1))
        ps = ctx.enter_context(tc.psum_pool(name="ps", bufs=1))

        def tile(name, shape, dtype=F32, tag=None):
            return sb.tile(shape, dtype, name=name, tag=tag or name, align_bytes=64)

        list_b = tile("list_b", [P, J // 16], U16)
        list_a = tile("list_a", [P, I // 16], U16)
        words = tile("words", [P, U], U16)
        scale_rows = tile("scale_rows", [P, U], U8)
        ident = tile("ident", [P, P])

        nc.gpsimd.memset(scale_rows[:].bitcast(I32), 0)
        nc.sync.dma_start(list_b[:], offs2)
        nc.sync.dma_start(out=words[:].bitcast(I32), in_=tabb_words[0].bitcast(I32))
        for r in range(4):
            nc.sync.dma_start(out=scale_rows[:].bitcast(I32)[r:P:32, :], in_=tabb_scales[0].bitcast(I32)[r:16:4, :])
        nc.sync.dma_start(list_a[:], offs)

        planes = {}
        for name, table in (("a", taba), ("d", dtab)):
            rows = table.rearrange("(p t) c -> p t c", t=PACK)
            for t in range(PACK):
                planes[name, t] = tile("plane_%s%d" % (name, t), [P, T])
                nc.sync.dma_start(out=planes[name, t][:], in_=rows[:, t, :])
            if name == "a":
                gw_sb = tile("gw_sb", [P, ROW_TILES, G])
                nc.sync.dma_start(out=gw_sb[:], in_=gw.rearrange("(r p) g -> p r g", p=P))
        base_sb = []
        for rt in range(ROW_TILES):
            base_sb.append(tile("base%d" % rt, [P, J]))
            nc.sync.dma_start(out=base_sb[rt][:], in_=base[rt * P : (rt + 1) * P, :])
        make_identity(nc, ident[:])

        listed_words = tile("listed_words", [P, J], U16)
        b_words = tile("b_words", [P, J], U16)
        b_scales = tile("b_scales", [P, J], U8)
        nc.vector.tensor_copy(listed_words[:], words[:].indirect(list_b[:]))
        nc.vector.tensor_copy(
            b_scales[:].rearrange("p (c g h) -> p g c h", c=C, h=H), scale_rows[:].indirect(list_b[:])
        )
        nc.vector.tensor_copy(
            out=b_words[:].rearrange("p (c g h) -> p c g h", c=C, h=H),
            in_=listed_words[:].rearrange("p (g c h) -> p c g h", c=C, h=H),
        )

        def listed(name, t, lo=0, hi=I):
            return planes[name, t][:].indirect(list_a[:, lo // 16 : hi // 16])

        def weave(name, picked, rt):
            woven = tile("woven_%s%d" % (name, rt), [P, P, PACK], BF16)
            nc.vector.tensor_copy(
                out=woven[:].rearrange("p (c i) t -> p c t i", i=4),
                in_=picked[:, :, rt * P : (rt + 1) * P].rearrange("p t (c i) -> p c t i", i=4),
            )
            return woven

        def quantise(name, woven):
            codes = tile("codes_" + name, [P, P], U32)
            scales = tile("scales_" + name, [P, P], U8)
            nc.vector.quantize_mx(
                out=codes[:].bitcast(FP8X4), scales=scales[:], in_=woven[:].rearrange("p i t -> p (i t)")
            )
            return codes, scales

        def turn(dst, src, start, stop):
            nc.tensor.matmul(dst, lhsT=src, rhs=ident[:], is_transpose=True, start=start, stop=stop)

        def chunk(ap, c):
            return ap[:, c * P : (c + 1) * P]

        def twice(ap):
            return ap.unsqueeze(2).to_broadcast([P, G, H])

        def over_chunks(ap):
            return ap.unsqueeze(1).to_broadcast([P, C, P])

        def by_chunk(ap):
            return ap.rearrange("p (c i) -> p c i", c=C)

        rows = [dict() for rt in range(ROW_TILES)]

        picked_a = tile("picked_a", [P, PACK, I], BF16)
        nc.scalar.activation(picked_a[:, 0, :], listed("a", 0), ACT.Copy)
        nc.vector.tensor_copy(picked_a[:, 1, :], listed("a", 1))
        nc.scalar.activation(picked_a[:, 2, :], listed("a", 2), ACT.Copy)
        nc.vector.tensor_copy(picked_a[:, 3, 0:P], listed("a", 3, 0, P))
        nc.scalar.activation(picked_a[:, 3, P:I], listed("a", 3, P, I), ACT.Copy)
        for rt, f in enumerate(rows):
            f["woven_a"] = weave("a", picked_a, rt)
        for rt, f in enumerate(rows):
            f["gain_gw"] = tile("gain_gw%d" % rt, [P, G])
            f["gw_sum"] = tile("gw_sum%d" % rt, [P, 1])
            nc.scalar.activation(
                out=f["gain_gw"][:], in_=gw_sb[:, rt, :], func=ACT.Copy, scale=GAIN, accum_out=f["gw_sum"][:]
            )
        picked_d = tile("picked_d", [P, PACK, I], BF16)
        for rt, f in enumerate(rows):
            codes, scales = quantise("a%d" % rt, f["woven_a"])
            f["s"] = ps.tile([P, J], F32, name="s%d" % rt, tag="wide%d" % rt)
            nc.tensor.matmul_mx(
                out=f["s"][:], lhsT=codes[:].bitcast(FP8X4), lhsT_scale=scales[:],
                rhs=b_words[:].bitcast(FP4X4), rhs_scale=b_scales[:], start=True, stop=True,
            )
        nc.scalar.activation(picked_d[:, 0, :], listed("d", 0), ACT.Copy)
        for rt, f in enumerate(rows):
            nc.scalar.activation(picked_d[:, 1 + rt, :], listed("d", 1 + rt), ACT.Copy)
            neg_max = tile("neg_max%d" % rt, [P, 1])[:]
            nc.vector.tensor_reduce(out=neg_max, in_=f["s"][:], axis=AX.X, op=ALU.max, negate=True)
            f["p"] = tile("p%d" % rt, [P, J], tag="plane_d%d" % (1 + rt))
            f["den"] = tile("den%d" % rt, [P, G + 1])
            nc.scalar.activation(
                out=f["p"][:], in_=f["s"][:], func=ACT.Exp, bias=neg_max, accum_out=f["den"][:, G : G + 1]
            )
            f["p_turned"] = ps.tile([P, J], F32, name="p_turned%d" % rt, tag="mid%d" % rt)
            for c in range(C):
                turn(chunk(f["p_turned"], c), chunk(f["p"], c), True, True)
        nc.vector.tensor_copy(picked_d[:, 3, :], listed("d", 3))
        for rt, f in enumerate(rows):
            f["woven_d"] = weave("d", picked_d, rt)
        for rt, f in enumerate(rows):
            f["pT"] = tile("pT%d" % rt, [P, J])[:]
            nc.scalar.copy(out=f["pT"], in_=f["p_turned"][:])
        for rt, f in enumerate(rows):
            codes, scales = quantise("d%d" % rt, f["woven_d"])
            f["ts"] = ps.tile([P, J], F32, name="ts%d" % rt)
            for c in range(C):
                nc.tensor.matmul_mx(
                    out=chunk(f["ts"], c), lhsT=chunk(b_words, c).bitcast(FP4X4), lhsT_scale=chunk(b_scales, c),
                    rhs=codes[:].bitcast(FP8X4), rhs_scale=scales[:], start=True, stop=True,
                )
        for rt, f in enumerate(rows):
            f["neg_s1"] = tile("neg_s1_%d" % rt, [P, G], tag=("neg_s1_0", "picked_d")[rt])[:]
            nc.vector.tensor_reduce(
                out=f["neg_s1"], in_=f["p"][:].rearrange("p (c g h) -> p g c h", c=C, h=H),
                axis=AX.XY, op=ALU.add, negate=True,
            )
            nc.vector.scalar_tensor_tensor(
                out=f["den"][:, 0:G], in0=f["den"][:, G : G + 1].to_broadcast([P, G]), scalar=EPS,
                in1=f["neg_s1"], op0=ALU.mult, op1=ALU.subtract,
            )
        for rt, f in enumerate(rows):
            root = tile("root%d" % rt, [P, G + 1], tag="codes_d%d" % rt)
            nc.scalar.activation(out=root[:], in_=f["den"][:], func=ACT.Abs_reciprocal_sqrt)
            f["inv"] = tile("inv%d" % rt, [P, G + 1])
            nc.scalar.activation(out=f["inv"][:], in_=root[:], func=ACT.Square)
        for rt, f in enumerate(rows):
            f["xpT"] = tile("xpT%d" % rt, [P, J])
            nc.vector.tensor_tensor(out=f["xpT"][:], in0=f["ts"][:], in1=f["pT"], op=ALU.mult)
            f["pairs"] = ps.tile([P, P], F32, name="pairs%d" % rt, tag="mid%d" % rt)
            for c in range(C):
                turn(f["pairs"][:], chunk(f["xpT"], c), c == 0, c == C - 1)
        for rt, f in enumerate(rows):
            f["pair_sums"] = tile("pair_sums%d" % rt, [P, G, H])
            xz = tile("xz%d" % rt, [P, 1])
            nc.scalar.activation(
                out=f["pair_sums"][:].rearrange("p g h -> p (g h)"), in_=f["pairs"][:], func=ACT.Copy, accum_out=xz[:]
            )
            f["xz_eps"] = tile("xz_eps%d" % rt, [P, 1])
            nc.scalar.activation(out=f["xz_eps"][:], in_=xz[:], func=ACT.Copy, scale=EPS)
            f["xz_gw"] = tile("xz_gw%d" % rt, [P, 1])
            nc.scalar.activation(out=f["xz_gw"][:], in_=xz[:], func=ACT.Copy, scale=f["gw_sum"][:])
        for rt, f in enumerate(rows):
            f["w"] = tile("w%d" % rt, [P, G, H])
            nc.vector.tensor_tensor(
                out=f["w"][:], in0=twice(f["gain_gw"][:]), in1=twice(f["inv"][:, 0:G]), op=ALU.mult
            )
        for rt, f in enumerate(rows):
            f["curv"] = tile("curv%d" % rt, [P, G])
            nc.vector.tensor_tensor(out=f["curv"][:], in0=f["w"][:, :, 0], in1=f["inv"][:, 0:G], op=ALU.mult)
            terms = tile("mean_terms%d" % rt, [P, G])
            neg_mean = tile("neg_mean%d" % rt, [P, 1])
            nc.vector.scalar_tensor_tensor(
                out=terms[:], in0=f["w"][:, :, 0], scalar=f["inv"][:, G : G + 1], in1=f["neg_s1"],
                op0=ALU.mult, op1=ALU.mult, accum_out=neg_mean[:],
            )
            f["bT"] = ps.tile([P, P], F32, name="bT%d" % rt)
            turn(f["bT"][:], f["w"][:].rearrange("p g h -> p (g h)"), True, False)
            turn(f["bT"][:], neg_mean[:].to_broadcast([P, P]), False, True)
        for rt, f in enumerate(rows):
            f["first"] = tile("first%d" % rt, [P, J])
            f["x_den"] = f["first"][:, 0:G]
            nc.vector.scalar_tensor_tensor(
                out=f["x_den"], in0=f["pair_sums"][:, :, 0], scalar=f["xz_eps"][:], in1=f["pair_sums"][:, :, 1],
                op0=ALU.add, op1=ALU.add,
            )
        for rt, f in enumerate(rows):
            inv_z = f["inv"][:, G : G + 1]
            f["xz_k"] = tile("xz_k%d" % rt, [P, 1])
            nc.vector.tensor_scalar(
                out=f["xz_k"][:], in0=f["xz_gw"][:], scalar1=inv_z, scalar2=inv_z, op0=ALU.mult, op1=ALU.mult
            )
            f["y"] = tile("y%d" % rt, [P, G, H])
            f["y_sum"] = tile("y_sum%d" % rt, [P, 1])
            nc.vector.scalar_tensor_tensor(
                out=f["y"][:], in0=twice(f["x_den"]), scalar=-1.0, in1=twice(f["curv"][:]),
                op0=ALU.mult, op1=ALU.mult, accum_out=f["y_sum"][:],
            )
        for rt, f in enumerate(rows):
            shift = tile("shift%d" % rt, [P, 1])
            nc.vector.tensor_scalar(
                out=shift[:], in0=f["y_sum"][:], scalar1=EPS / H, scalar2=f["xz_k"][:], op0=ALU.mult, op1=ALU.add
            )
            f["dT"] = ps.tile([P, P], F32, name="dT%d" % rt, tag="mid%d" % rt)
            turn(f["dT"][:], f["y"][:].rearrange("p g h -> p (g h)"), True, False)
            turn(f["dT"][:], shift[:].to_broadcast([P, P]), False, True)
        for rt, f in enumerate(rows):
            first = f["first"]
            nc.vector.tensor_tensor(
                out=by_chunk(first[:]), in0=over_chunks(f["bT"][:]), in1=by_chunk(f["xpT"][:]), op=ALU.mult
            )
            f["total"] = ps.tile([P, J], F32, name="total%d" % rt, tag="wide%d" % rt)
            for c in range(C):
                turn(chunk(f["total"], c), chunk(first, c), c == 0, False)
            for lo in range(0, C, C // 2):
                second = tile("second%d_%d" % (rt, lo), [P, C // 2, P])
                nc.vector.tensor_tensor(
                    out=second[:], in0=over_chunks(f["dT"][:])[:, lo : lo + C // 2, :],
                    in1=by_chunk(f["pT"])[:, lo : lo + C // 2, :], op=ALU.mult,
                )
                for c in range(lo, lo + C // 2):
                    turn(chunk(f["total"], c), second[:, c - lo, :], False, c == C - 1)
        for rt, f in enumerate(rows):
            for half, queue in enumerate((nc.sync, nc.scalar)):
                groups = slice(half * G // 2, (half + 1) * G // 2)
                cols = slice(half * J // 2, (half + 1) * J // 2)
                result = tile("result%d_%d" % (rt, half), [P, J // 2])
                nc.vector.tensor_tensor(
                    out=result[:].rearrange("p (g c h) -> p g c h", c=C, h=H),
                    in0=f["total"][:].rearrange("p (c g h) -> p g c h", c=C, h=H)[:, groups],
                    in1=base_sb[rt][:, cols].rearrange("p (g c h) -> p g c h", c=C, h=H),
                    op=ALU.add,
                )
                queue.dma_start(out=out[rt * P : (rt + 1) * P, cols], in_=result[:])
